import numpy as np
import ml_dtypes


def mxq(x, axis, fmt="e4m3"):
    dtype, down = {"e4m3": (ml_dtypes.float8_e4m3fn, 7), "e5m2": (ml_dtypes.float8_e5m2, 14)}[fmt]
    v = np.moveaxis(np.asarray(x, np.float32).astype(ml_dtypes.bfloat16).astype(np.float64), axis, -1)
    blocks = v.reshape(v.shape[:-1] + (-1, 32))
    amax = np.abs(blocks).max(-1, keepdims=True)
    byte = np.maximum(np.where(amax > 0, np.frexp(amax)[1] - 1 + 127, 0) - down, 1)
    scale = np.exp2(byte - 127.0)
    codes = (blocks / scale).astype(np.float32).astype(dtype).astype(np.float64)
    return np.moveaxis((codes * scale).reshape(v.shape), -1, axis)


WIDE = False


def mx_kscale(k):
    if not WIDE:
        return np.ones(k)
    levels = np.array([10, -10, 5, -5, 0])
    if k % 512:
        return np.exp2(np.random.permutation(np.resize(levels, k // 32))).repeat(32)
    a = np.empty((k // 512, 16))
    for p in range(k // 512):
        a[p, :8] = np.random.permutation(np.resize(levels, 8))
        for g in range(8):
            far = levels[np.abs(levels - a[p, g]) >= 10]
            a[p, g + 8] = far[np.random.randint(len(far))]
    return np.exp2(a.ravel()).repeat(32)


def f64(x):
    return np.asarray(x).astype(np.float64)


def striped(idx):
    return np.tile(idx.reshape(-1, 16).T, (8, 1)).astype(np.uint16)


def unstriped(offs):
    return offs[:16].T.reshape(-1).astype(np.int64)


def pack_weight(w):
    k, n = w.shape
    w = f64(np.asarray(w, np.float32).astype(ml_dtypes.bfloat16)).reshape(k // 32, 32, n)
    amax = np.abs(w).max(1)
    byte = np.clip(np.where(amax > 0, np.frexp(amax)[1] - 1 + 127 - 7, 1), 1, 254)
    scaled = (w * np.exp2(127.0 - byte)[:, None, :]).reshape(k, n).astype(np.float32)
    words = np.ascontiguousarray(scaled.reshape(k // 512, 128, 4, n).transpose(0, 1, 3, 2)).astype(ml_dtypes.float8_e4m3fn).view(np.uint8)
    return words, np.ascontiguousarray(byte.astype(np.uint8).reshape(k // 512, 16, n))


def unpack_weight(words, scales):
    g, p, n, _ = words.shape
    vals = np.ascontiguousarray(words).view(ml_dtypes.float8_e4m3fn).astype(np.float64) * np.repeat(np.exp2(scales.astype(np.float64) - 127.0), 8, axis=1)[..., None]
    return vals.transpose(0, 1, 3, 2).reshape(g * 512, n)


K, T, S, N, H, W, G = 512, 2048, 512, 512, 512, 256, 2048


def setup_inputs():
    n = np.random.standard_normal
    s = mx_kscale(K)[:, None]
    u = mx_kscale(H)
    packed_xT = pack_weight(n((K, T)) * s)
    perm = np.random.permutation(S)
    return {
        "x_words": packed_xT[0],
        "x_scales": packed_xT[1],
        "w1": (n((K, H)) / np.sqrt(K) / s).astype(np.float32),
        "gn": (np.random.uniform(0.5, 1.5, (H, 1)) * u[:, None]).astype(np.float32),
        "w2": (n((H, N)) / np.sqrt(H) / u[:, None]).astype(np.float32),
        "tau": np.random.uniform(0.3, 0.9, (N, 1)).astype(np.float32),
        "offs": striped(np.random.permutation(T)[:S]),
        "n1": striped(perm[:W]),
        "n2": striped(perm[W:]),
        "n3": striped(np.random.randint(0, S, G)),
    }


def reference(x_words, x_scales, w1, gn, w2, tau, offs, n1, n2, n3):
    xq = unpack_weight(x_words, x_scales)[:, unstriped(offs)]
    y = mxq(f64(w1), 0, "e4m3").T @ xq
    pa = y[:, unstriped(n1)]
    pb = y[:, unstriped(n2)]
    rb = np.minimum(pa, pb)
    ra = np.maximum(pa, pb)
    ds = np.zeros((H, S))
    ds[:, unstriped(n1)] = ra
    dt = ds.copy()
    dt[:, unstriped(n2)] = rb
    z = f64(gn) * dt
    h = mxq(f64(w2), 0, "e4m3").T @ mxq(z, 0, "e4m3")
    top = h.max(axis=1, keepdims=True)
    ea = np.exp(f64(tau) * (h[:, unstriped(n3)] - top))
    ms = ea.reshape(N, S, 4).sum(axis=2)
    return (1.5 * h) / (ms + 0.5)

@@ -1,0 +1,269 @@
+from contextlib import ExitStack
+
+import concourse.mybir as mybir
+
+K, T, S, N, H, W, G = 512, 2048, 512, 512, 512, 256, 2048
+FLOPS = 2 * K * H * S + 2 * H * N * S
+
+F32 = mybir.dt.float32
+BF16 = mybir.dt.bfloat16
+I32 = mybir.dt.int32
+U32 = mybir.dt.uint32
+U16 = mybir.dt.uint16
+U8 = mybir.dt.uint8
+FP8X4 = mybir.dt.float8_e4m3fn_x4
+ALU = mybir.AluOpType
+ACT = mybir.ActivationFunctionType
+
+P = 128
+PACK = 4
+MEMBERS = 4
+PIECE = 512
+
+
+def tile_picked_layorderegs_none_p_kernel(
+    tc, x_words, x_scales, w1, gn, w2, tau, offs, n1, n2, n3, out
+):
+    nc = tc.nc
+    with ExitStack() as ctx:
+        keep = ctx.enter_context(tc.tile_pool(name="keep", bufs=1))
+        ring = ctx.enter_context(tc.tile_pool(name="ring", bufs=2))
+        psum = ctx.enter_context(tc.psum_pool(name="psum", bufs=1))
+
+        offs_sb = keep.tile([P, S // 16], U16, name="offs_sb")
+        n1_sb = keep.tile([P, W // 16], U16, name="n1_sb")
+        n2_sb = keep.tile([P, W // 16], U16, name="n2_sb")
+        n3_sb = keep.tile([P, G // 16], U16, name="n3_sb")
+        xw = keep.tile([P, T], I32, name="xw", align_bytes=64)
+        xs = keep.tile([P, T], U8, name="xs", align_bytes=64)
+        gn_sb = keep.tile([P, PACK], F32, name="gn_sb")
+        tau_sb = keep.tile([P, PACK], F32, name="tau_sb")
+        half = H // 2
+        w1_raw = [keep.tile([P, PACK, half], F32, name=f"w1_raw{u}") for u in range(2)]
+        w2_first = keep.tile([P, PACK, P], F32, name="w2_first")
+        w2_rest = keep.tile([P, PACK, N - P], F32, name="w2_rest")
+
+        nc.vector.memset(xs[:].bitcast(I32), 0)
+        nc.sync.dma_start(xw[:], x_words[0].rearrange("p n t -> p (n t)").bitcast(I32))
+        nc.sync.dma_start(offs_sb[:], offs)
+        for q in range(4):
+            nc.scalar.dma_start(
+                xs[32 * q : 32 * q + 4, :].bitcast(I32), x_scales[0, 4 * q : 4 * q + 4, :].bitcast(I32)
+            )
+        w1_rows = w1.rearrange("(p j) c -> p j c", j=PACK)
+        for u in range(2):
+            nc.sync.dma_start(w1_raw[u][:], w1_rows[:, :, u * half : (u + 1) * half])
+        w2_rows = w2.rearrange("(p j) c -> p j c", j=PACK)
+        nc.sync.dma_start(w2_first[:], w2_rows[:, :, :P])
+        nc.sync.dma_start(n1_sb[:], n1)
+        nc.sync.dma_start(n2_sb[:], n2)
+        nc.sync.dma_start(gn_sb[:], gn.rearrange("(p t) o -> p (t o)", t=PACK))
+        nc.sync.dma_start(w2_rest[:], w2_rows[:, :, P:])
+        nc.sync.dma_start(n3_sb[:], n3)
+        with nc.allow_non_contiguous_dma(reason="one rate a partition for each block of 128 rows"):
+            nc.sync.dma_start(tau_sb[:], tau.rearrange("(b p) o -> p (b o)", p=P))
+
+        xq_words = keep.tile([P, S], U32, name="xq_words", align_bytes=64)
+        xq_scales = keep.tile([P, S], U8, name="xq_scales", align_bytes=64)
+        nc.vector.tensor_copy(xq_words[:], xw[:].bitcast(U32).indirect(offs_sb[:]))
+        nc.vector.tensor_copy(xq_scales[:], xs[:].indirect(offs_sb[:]))
+
+        w1_bf = keep.tile([P, PACK, P, PACK], BF16, name="w1_bf", align_bytes=64)
+        for u, copy in enumerate((nc.scalar.copy, nc.vector.tensor_copy)):
+            copy(
+                w1_bf[:, :, u * 64 : (u + 1) * 64, :].rearrange("p t m j -> p m j t"),
+                w1_raw[u][:].rearrange("p j (m t) -> p m j t", t=PACK),
+            )
+        w1_words = keep.tile([P, H], U32, name="w1_words", align_bytes=64)
+        w1_scales = keep.tile([P, H], U8, name="w1_scales", align_bytes=64)
+        for t in range(PACK):
+            cols = slice(t * P, (t + 1) * P)
+            nc.vector.quantize_mx(
+                out=w1_words[:, cols].bitcast(FP8X4),
+                scales=w1_scales[:, cols],
+                in_=w1_bf[:, t, :, :].rearrange("p m j -> p (m j)"),
+            )
+
+        w2_words = [keep.tile([P, P], U32, name=f"w2_words{b}", align_bytes=64) for b in range(PACK)]
+        w2_scales = [keep.tile([P, P], U8, name=f"w2_scales{b}", align_bytes=64) for b in range(PACK)]
+
+        def round_w2(grouped, raw):
+            nc.scalar.copy(
+                grouped.rearrange("p (c i) j -> p c j i", i=4), raw.rearrange("p j (c i) -> p c j i", i=4)
+            )
+
+        def quantise_w2(b, grouped):
+            nc.vector.quantize_mx(
+                out=w2_words[b][:].bitcast(FP8X4), scales=w2_scales[b][:], in_=grouped.rearrange("p m j -> p (m j)")
+            )
+
+        w2_bf_first = keep.tile([P, P, PACK], BF16, name="w2_bf_first", align_bytes=64)
+        round_w2(w2_bf_first[:], w2_first[:])
+
+        banks = [psum.tile([P, S], F32, name=f"bank{b}") for b in range(8)]
+        rows = [keep.tile([P, 2 * S], F32, name=f"rows{t}") for t in range(PACK)]
+        z_planes = keep.tile([P, PACK, S], BF16, name="z_planes", tag="late_bf16", align_bytes=64)
+
+        for t in range(PACK):
+            cols = slice(t * P, (t + 1) * P)
+            nc.tensor.matmul_mx(
+                out=banks[t][:],
+                lhsT=w1_words[:, cols].bitcast(FP8X4),
+                lhsT_scale=w1_scales[:, cols],
+                rhs=xq_words[:].bitcast(FP8X4),
+                rhs_scale=xq_scales[:],
+                start=True,
+                stop=True,
+            )
+            nc.scalar.copy(rows[t][:, S:], banks[t][:])
+
+        sorted_rows = []
+        for t in range(PACK):
+            y = rows[t][:, S:]
+            pa = ring.tile([P, W], F32, name="pa")
+            pb = ring.tile([P, W], F32, name="pb")
+            ra = keep.tile([P, W], F32, name=f"ra{t}")
+            rb = keep.tile([P, W], F32, name=f"rb{t}")
+            nc.vector.tensor_copy(pa[:], y.indirect(n1_sb[:]))
+            nc.vector.tensor_copy(pb[:], y.indirect(n2_sb[:]))
+            nc.vector.tensor_tensor(ra[:], pa[:], pb[:], ALU.max)
+            nc.vector.tensor_tensor(rb[:], pa[:], pb[:], ALU.min)
+            dt = keep.tile([P, S], F32, name=f"dt{t}")
+            if t < PACK - 1:
+                nc.scalar.activation(dt[:].indirect(n1_sb[:]), ra[:], ACT.Copy)
+                nc.scalar.activation(dt[:].indirect(n2_sb[:]), rb[:], ACT.Copy)
+            else:
+                nc.vector.tensor_copy(dt[:].indirect(n1_sb[:]), ra[:])
+                nc.vector.tensor_copy(dt[:].indirect(n2_sb[:]), rb[:])
+            sorted_rows.append(dt)
+        quantise_w2(0, w2_bf_first[:])
+        neg_tau = keep.tile([P, PACK], F32, name="neg_tau")
+        nc.vector.tensor_scalar(neg_tau[:], tau_sb[:], -1.0, None, ALU.mult)
+        for t in (0, 1, 3):
+            nc.vector.tensor_scalar(z_planes[:, t, :], sorted_rows[t][:], gn_sb[:, t : t + 1], None, ALU.mult)
+        nc.vector.tensor_scalar(z_planes[:, 2, :half], sorted_rows[2][:, :half], gn_sb[:, 2:3], None, ALU.mult)
+        nc.scalar.activation(z_planes[:, 2, half:], sorted_rows[2][:, half:], ACT.Copy, scale=gn_sb[:, 2:3])
+
+        z_bf = keep.tile([P, S, PACK], BF16, name="z_bf", align_bytes=64)
+        z_words = [keep.tile([P, half], U32, name=f"z_words{u}", align_bytes=64) for u in range(2)]
+        z_scales = [keep.tile([P, half], U8, name=f"z_scales{u}", align_bytes=64) for u in range(2)]
+        for u, copy in enumerate((nc.vector.tensor_copy, nc.scalar.copy)):
+            cols = slice(u * half, (u + 1) * half)
+            copy(
+                z_bf[:, cols, :].rearrange("p (c i) t -> p c t i", i=4),
+                z_planes[:, :, cols].rearrange("p t (c i) -> p c t i", i=4),
+            )
+        for u in range(2):
+            cols = slice(u * half, (u + 1) * half)
+            nc.vector.quantize_mx(
+                out=z_words[u][:].bitcast(FP8X4),
+                scales=z_scales[u][:],
+                in_=z_bf[:, cols, :].rearrange("p c t -> p (c t)"),
+            )
+
+        top = keep.tile([P, PACK, 2], F32, name="top")
+        bias = keep.tile([P, PACK], F32, name="bias")
+
+        def second_product(b):
+            for u in range(2):
+                bank = banks[2 * b + u]
+                nc.tensor.matmul_mx(
+                    out=bank[:, :half],
+                    lhsT=w2_words[b][:].bitcast(FP8X4),
+                    lhsT_scale=w2_scales[b][:],
+                    rhs=z_words[u][:].bitcast(FP8X4),
+                    rhs_scale=z_scales[u][:],
+                    start=True,
+                    stop=True,
+                )
+                nc.vector.tensor_scalar(
+                    rows[b][:, u * half : (u + 1) * half],
+                    bank[:, :half],
+                    1.0,
+                    None,
+                    ALU.mult,
+                    ALU.max,
+                    accum_out=top[:, b, u : u + 1],
+                )
+            nc.vector.tensor_scalar(
+                bias[:, b : b + 1], top[:, b, 0:1], top[:, b, 1:2], neg_tau[:, b : b + 1], ALU.max, ALU.mult
+            )
+
+        second_product(0)
+        w2_bf_rest = keep.tile([P, N - P, PACK], BF16, name="w2_bf_rest", tag="late_bf16", align_bytes=64)
+        for b in range(1, PACK):
+            cols = slice((b - 1) * P, b * P)
+            round_w2(w2_bf_rest[:, cols, :], w2_rest[:, :, cols])
+        for b in range(1, PACK):
+            quantise_w2(b, w2_bf_rest[:, (b - 1) * P : b * P, :])
+        for b in range(1, PACK):
+            second_product(b)
+
+        per = PIECE // MEMBERS
+        pieces = G // PIECE
+        out_rows = out.rearrange("(b p) j -> p b j", p=P)
+        pair_sums = [keep.tile([P, S, 2], F32, name=f"pair_sums{b}") for b in range(PACK)]
+
+        def members(b, c):
+            ea = ring.tile([P, per, MEMBERS], F32, name="ea", bufs=4)
+            nc.scalar.activation(
+                ea[:].rearrange("p j t -> p (j t)"),
+                rows[b][:].indirect(n3_sb[:, c * PIECE // 16 : (c + 1) * PIECE // 16]),
+                ACT.Exp,
+                bias=bias[:, b : b + 1],
+                scale=tau_sb[:, b : b + 1],
+            )
+            nc.vector.tensor_tensor(pair_sums[b][:, c * per : (c + 1) * per, :], ea[:, :, 0:2], ea[:, :, 2:4], ALU.add)
+
+        def next_members(b, c):
+            if b + 1 < PACK:
+                members(b + 1, c)
+
+        for c in range(pieces):
+            members(0, c)
+        for b in range(PACK):
+            den = [ring.tile([P, 2, 128], F32, name=f"den{u}") for u in range(2)]
+            prod2 = [ring.tile([P, 2, 64], F32, name=f"prod2{u}") for u in range(2)]
+            prod4 = [ring.tile([P, 64], F32, name=f"prod4{u}") for u in range(2)]
+            inv4 = [ring.tile([P, 64], F32, name=f"inv4{u}") for u in range(2)]
+            inv2 = [ring.tile([P, 2, 64], F32, name=f"inv2{u}") for u in range(2)]
+            inv1 = [ring.tile([P, 2, 128], F32, name=f"inv1{u}") for u in range(2)]
+            res = ring.tile([P, S], F32, name="res")
+            for u in range(2):
+                sums = pair_sums[b][:, u * half : (u + 1) * half, :]
+                nc.vector.scalar_tensor_tensor(
+                    den[u][:].rearrange("p v j -> p (v j)"), sums[:, :, 0], 0.5, sums[:, :, 1], ALU.add, ALU.add
+                )
+            for u in range(2):
+                nc.vector.tensor_tensor(
+                    prod2[u][:].rearrange("p v j -> p (v j)"), den[u][:, 0, :], den[u][:, 1, :], ALU.mult
+                )
+            next_members(b, 0)
+            for u in range(2):
+                nc.vector.tensor_tensor(prod4[u][:], prod2[u][:, 0, :], prod2[u][:, 1, :], ALU.mult)
+            for u in range(2):
+                nc.vector.reciprocal(inv4[u][:], prod4[u][:])
+            for u in range(2):
+                nc.vector.tensor_tensor(
+                    inv2[u][:], prod2[u][:, ::-1, :], inv4[u][:].unsqueeze(1).to_broadcast([P, 2, 64]), ALU.mult
+                )
+            next_members(b, 1)
+            for u in range(2):
+                nc.vector.tensor_tensor(
+                    inv1[u][:],
+                    den[u][:, ::-1, :],
+                    inv2[u][:].rearrange("p v j -> p (v j)").unsqueeze(1).to_broadcast([P, 2, 128]),
+                    ALU.mult,
+                )
+            for u in range(2):
+                nc.vector.scalar_tensor_tensor(
+                    res[:, u * half : (u + 1) * half],
+                    banks[2 * b + u][:, :half],
+                    1.5,
+                    inv1[u][:].rearrange("p v j -> p (v j)"),
+                    ALU.mult,
+                    ALU.mult,
+                )
+                nc.sync.dma_start(out_rows[:, b, u * half : (u + 1) * half], res[:, u * half : (u + 1) * half])
+            next_members(b, 2)
+            next_members(b, 3)

@@ -34,49 +34,33 @@ def tile_picked_layorderegs_none_p_kernel(
         n1_sb = keep.tile([P, W // 16], U16, name="n1_sb")
         n2_sb = keep.tile([P, W // 16], U16, name="n2_sb")
         n3_sb = keep.tile([P, G // 16], U16, name="n3_sb")
-        xw = keep.tile([P, T], I32, name="xw", align_bytes=64)
+        xw = keep.tile([P, T], I32, name="xw", tag="x_then_w2", align_bytes=64)
         xs = keep.tile([P, T], U8, name="xs", align_bytes=64)
-        gn_sb = keep.tile([P, PACK], F32, name="gn_sb")
-        tau_sb = keep.tile([P, PACK], F32, name="tau_sb")
         half = H // 2
-        w1_raw = [keep.tile([P, PACK, half], F32, name=f"w1_raw{u}") for u in range(2)]
-        w2_first = keep.tile([P, PACK, P], F32, name="w2_first")
-        w2_rest = keep.tile([P, PACK, N - P], F32, name="w2_rest")
+        w1_raw = keep.tile([P, PACK, H], F32, name="w1_raw", tag="w1_then_w2")
 
         nc.vector.memset(xs[:].bitcast(I32), 0)
-        nc.sync.dma_start(xw[:], x_words[0].rearrange("p n t -> p (n t)").bitcast(I32))
         nc.sync.dma_start(offs_sb[:], offs)
+        nc.sync.dma_start(n1_sb[:], n1)
+        nc.sync.dma_start(w1_raw[:], w1.rearrange("(p j) c -> p j c", j=PACK))
         for q in range(4):
-            nc.scalar.dma_start(
+            nc.sync.dma_start(
                 xs[32 * q : 32 * q + 4, :].bitcast(I32), x_scales[0, 4 * q : 4 * q + 4, :].bitcast(I32)
             )
-        w1_rows = w1.rearrange("(p j) c -> p j c", j=PACK)
-        for u in range(2):
-            nc.sync.dma_start(w1_raw[u][:], w1_rows[:, :, u * half : (u + 1) * half])
-        w2_rows = w2.rearrange("(p j) c -> p j c", j=PACK)
-        nc.sync.dma_start(w2_first[:], w2_rows[:, :, :P])
-        nc.sync.dma_start(n1_sb[:], n1)
         nc.sync.dma_start(n2_sb[:], n2)
-        nc.sync.dma_start(gn_sb[:], gn.rearrange("(p t) o -> p (t o)", t=PACK))
-        nc.sync.dma_start(w2_rest[:], w2_rows[:, :, P:])
         nc.sync.dma_start(n3_sb[:], n3)
-        with nc.allow_non_contiguous_dma(reason="one rate a partition for each block of 128 rows"):
-            nc.sync.dma_start(tau_sb[:], tau.rearrange("(b p) o -> p (b o)", p=P))
+        nc.sync.dma_start(xw[:], x_words[0].rearrange("p n t -> p (n t)").bitcast(I32))
 
-        xq_words = keep.tile([P, S], U32, name="xq_words", align_bytes=64)
-        xq_scales = keep.tile([P, S], U8, name="xq_scales", align_bytes=64)
-        nc.vector.tensor_copy(xq_words[:], xw[:].bitcast(U32).indirect(offs_sb[:]))
-        nc.vector.tensor_copy(xq_scales[:], xs[:].indirect(offs_sb[:]))
-
-        w1_bf = keep.tile([P, PACK, P, PACK], BF16, name="w1_bf", align_bytes=64)
+        w1_bf = keep.tile([P, PACK, P, PACK], BF16, name="w1_bf", tag="w1_then_rows", align_bytes=64)
         for u, copy in enumerate((nc.scalar.copy, nc.vector.tensor_copy)):
             copy(
                 w1_bf[:, :, u * 64 : (u + 1) * 64, :].rearrange("p t m j -> p m j t"),
-                w1_raw[u][:].rearrange("p j (m t) -> p m j t", t=PACK),
+                w1_raw[:, :, u * half : (u + 1) * half].rearrange("p j (m t) -> p m j t", t=PACK),
             )
         w1_words = keep.tile([P, H], U32, name="w1_words", align_bytes=64)
         w1_scales = keep.tile([P, H], U8, name="w1_scales", align_bytes=64)
-        for t in range(PACK):
+
+        def quantise_w1(t):
             cols = slice(t * P, (t + 1) * P)
             nc.vector.quantize_mx(
                 out=w1_words[:, cols].bitcast(FP8X4),
@@ -84,13 +68,34 @@ def tile_picked_layorderegs_none_p_kernel(
                 in_=w1_bf[:, t, :, :].rearrange("p m j -> p (m j)"),
             )
 
+        xq_words = keep.tile([P, S], U32, name="xq_words", align_bytes=64)
+        xq_scales = keep.tile([P, S], U8, name="xq_scales", align_bytes=64)
+        for t in range(PACK):
+            quantise_w1(t)
+        nc.vector.tensor_copy(xq_scales[:], xs[:].indirect(offs_sb[:]))
+        for u in range(2):
+            nc.vector.tensor_copy(
+                xq_words[:, u * half : (u + 1) * half],
+                xw[:].bitcast(U32).indirect(offs_sb[:, u * half // 16 : (u + 1) * half // 16]),
+            )
+
+        w2_rows = w2.rearrange("(p j) c -> p j c", j=PACK)
+        w2_first = keep.tile([P, PACK, P], F32, name="w2_first", tag="w1_then_w2")
+        w2_rest = keep.tile([P, PACK, N - P], F32, name="w2_rest", tag="x_then_w2", align_bytes=64)
+        per_row = keep.tile([P, 16], F32, name="per_row", tag="w1_then_rows", align_bytes=64)
+        gn_sb = per_row[:, 0:PACK]
+        tau_sb = per_row[:, 8 : 8 + PACK]
+        nc.sync.dma_start(w2_first[:], w2_rows[:, :, :P])
+        nc.sync.dma_start(gn_sb, gn.rearrange("(p t) o -> p (t o)", t=PACK))
+        with nc.allow_non_contiguous_dma(reason="one rate a partition for each block of 128 rows"):
+            nc.sync.dma_start(tau_sb, tau.rearrange("(b p) o -> p (b o)", p=P))
+        nc.sync.dma_start(w2_rest[:], w2_rows[:, :, P:])
+
         w2_words = [keep.tile([P, P], U32, name=f"w2_words{b}", align_bytes=64) for b in range(PACK)]
         w2_scales = [keep.tile([P, P], U8, name=f"w2_scales{b}", align_bytes=64) for b in range(PACK)]
 
-        def round_w2(grouped, raw):
-            nc.scalar.copy(
-                grouped.rearrange("p (c i) j -> p c j i", i=4), raw.rearrange("p j (c i) -> p c j i", i=4)
-            )
+        def round_w2(copy, grouped, raw):
+            copy(grouped.rearrange("p (c i) j -> p c j i", i=4), raw.rearrange("p j (c i) -> p c j i", i=4))
 
         def quantise_w2(b, grouped):
             nc.vector.quantize_mx(
@@ -98,49 +103,83 @@ def tile_picked_layorderegs_none_p_kernel(
             )
 
         w2_bf_first = keep.tile([P, P, PACK], BF16, name="w2_bf_first", align_bytes=64)
-        round_w2(w2_bf_first[:], w2_first[:])
+        round_w2(nc.scalar.copy, w2_bf_first[:], w2_first[:])
 
         banks = [psum.tile([P, S], F32, name=f"bank{b}") for b in range(8)]
         rows = [keep.tile([P, 2 * S], F32, name=f"rows{t}") for t in range(PACK)]
         z_planes = keep.tile([P, PACK, S], BF16, name="z_planes", tag="late_bf16", align_bytes=64)
 
-        for t in range(PACK):
-            cols = slice(t * P, (t + 1) * P)
+        def first_product(t, bank, cols):
+            rows_t = slice(t * P, (t + 1) * P)
             nc.tensor.matmul_mx(
-                out=banks[t][:],
-                lhsT=w1_words[:, cols].bitcast(FP8X4),
-                lhsT_scale=w1_scales[:, cols],
-                rhs=xq_words[:].bitcast(FP8X4),
-                rhs_scale=xq_scales[:],
+                out=bank,
+                lhsT=w1_words[:, rows_t].bitcast(FP8X4),
+                lhsT_scale=w1_scales[:, rows_t],
+                rhs=xq_words[:, cols].bitcast(FP8X4),
+                rhs_scale=xq_scales[:, cols],
                 start=True,
                 stop=True,
             )
-            nc.scalar.copy(rows[t][:, S:], banks[t][:])
 
-        sorted_rows = []
-        for t in range(PACK):
-            y = rows[t][:, S:]
-            pa = ring.tile([P, W], F32, name="pa")
-            pb = ring.tile([P, W], F32, name="pb")
-            ra = keep.tile([P, W], F32, name=f"ra{t}")
-            rb = keep.tile([P, W], F32, name=f"rb{t}")
-            nc.vector.tensor_copy(pa[:], y.indirect(n1_sb[:]))
-            nc.vector.tensor_copy(pb[:], y.indirect(n2_sb[:]))
-            nc.vector.tensor_tensor(ra[:], pa[:], pb[:], ALU.max)
-            nc.vector.tensor_tensor(rb[:], pa[:], pb[:], ALU.min)
-            dt = keep.tile([P, S], F32, name=f"dt{t}")
+        for u, copy in enumerate((nc.scalar.copy, nc.vector.tensor_copy)):
+            first_product(0, banks[u][:, :half], slice(u * half, (u + 1) * half))
+            copy(rows[0][:, S + u * half : S + (u + 1) * half], banks[u][:, :half])
+        for t in range(1, PACK):
+            first_product(t, banks[1 + t][:], slice(0, S))
+            nc.scalar.copy(rows[t][:, S:], banks[1 + t][:])
+
+        pa = [keep.tile([P, W], F32, name=f"pa{t}") for t in range(PACK)]
+        pb = [keep.tile([P, W], F32, name=f"pb{t}") for t in range(PACK)]
+        ra = [keep.tile([P, W], F32, name=f"ra{t}") for t in range(PACK)]
+        rb = [keep.tile([P, W], F32, name=f"rb{t}") for t in range(PACK)]
+        sorted_rows = [keep.tile([P, S], F32, name=f"dt{t}") for t in range(PACK)]
+
+        def fetch_a(t):
+            nc.vector.tensor_copy(pa[t][:], rows[t][:, S:].indirect(n1_sb[:]))
+
+        def fetch_b(t):
+            nc.vector.tensor_copy(pb[t][:], rows[t][:, S:].indirect(n2_sb[:]))
+
+        def put(t, values, places):
             if t < PACK - 1:
-                nc.scalar.activation(dt[:].indirect(n1_sb[:]), ra[:], ACT.Copy)
-                nc.scalar.activation(dt[:].indirect(n2_sb[:]), rb[:], ACT.Copy)
+                nc.scalar.activation(sorted_rows[t][:].indirect(places[:]), values[:], ACT.Copy)
             else:
-                nc.vector.tensor_copy(dt[:].indirect(n1_sb[:]), ra[:])
-                nc.vector.tensor_copy(dt[:].indirect(n2_sb[:]), rb[:])
-            sorted_rows.append(dt)
+                nc.vector.tensor_copy(sorted_rows[t][:].indirect(places[:]), values[:])
+
+        def larger(t):
+            nc.vector.tensor_tensor(ra[t][:], pa[t][:], pb[t][:], ALU.max)
+
+        def smaller(t):
+            nc.vector.tensor_tensor(rb[t][:], pa[t][:], pb[t][:], ALU.min)
+
+        def apply_gain(t):
+            nc.vector.tensor_scalar(z_planes[:, t, :], sorted_rows[t][:], gn_sb[:, t : t + 1], None, ALU.mult)
+
+        fetch_a(0)
+        for t in range(PACK):
+            fetch_b(t)
+            if t + 1 < PACK:
+                fetch_a(t + 1)
+            else:
+                smaller(t - 1)
+            larger(t)
+            if 0 < t < PACK - 1:
+                smaller(t - 1)
+        smaller(PACK - 1)
+        for t in range(PACK - 1):
+            put(t, ra[t], n1_sb)
+            if t > 0:
+                put(t - 1, rb[t - 1], n2_sb)
+        put(PACK - 2, rb[PACK - 2], n2_sb)
+        put(PACK - 1, ra[PACK - 1], n1_sb)
+        apply_gain(0)
+        put(PACK - 1, rb[PACK - 1], n2_sb)
+
         quantise_w2(0, w2_bf_first[:])
         neg_tau = keep.tile([P, PACK], F32, name="neg_tau")
-        nc.vector.tensor_scalar(neg_tau[:], tau_sb[:], -1.0, None, ALU.mult)
-        for t in (0, 1, 3):
-            nc.vector.tensor_scalar(z_planes[:, t, :], sorted_rows[t][:], gn_sb[:, t : t + 1], None, ALU.mult)
+        nc.gpsimd.tensor_scalar(neg_tau[:], tau_sb, -1.0, 0.0, ALU.mult, ALU.add)
+        apply_gain(1)
+        apply_gain(3)
         nc.vector.tensor_scalar(z_planes[:, 2, :half], sorted_rows[2][:, :half], gn_sb[:, 2:3], None, ALU.mult)
         nc.scalar.activation(z_planes[:, 2, half:], sorted_rows[2][:, half:], ACT.Copy, scale=gn_sb[:, 2:3])
 
@@ -161,7 +200,7 @@ def tile_picked_layorderegs_none_p_kernel(
                 in_=z_bf[:, cols, :].rearrange("p c t -> p (c t)"),
             )
 
-        top = keep.tile([P, PACK, 2], F32, name="top")
+        top = [keep.tile([P, 2], F32, name=f"top{b}", tag=f"top{b}", align_bytes=64) for b in range(PACK)]
         bias = keep.tile([P, PACK], F32, name="bias")
 
         def second_product(b):
@@ -183,21 +222,25 @@ def tile_picked_layorderegs_none_p_kernel(
                     None,
                     ALU.mult,
                     ALU.max,
-                    accum_out=top[:, b, u : u + 1],
+                    accum_out=top[b][:, u : u + 1],
                 )
             nc.vector.tensor_scalar(
-                bias[:, b : b + 1], top[:, b, 0:1], top[:, b, 1:2], neg_tau[:, b : b + 1], ALU.max, ALU.mult
+                bias[:, b : b + 1], top[b][:, 0:1], top[b][:, 1:2], neg_tau[:, b : b + 1], ALU.max, ALU.mult
             )
 
         second_product(0)
-        w2_bf_rest = keep.tile([P, N - P, PACK], BF16, name="w2_bf_rest", tag="late_bf16", align_bytes=64)
-        for b in range(1, PACK):
+        w2_bf_mid = keep.tile([P, 2 * P, PACK], BF16, name="w2_bf_mid", tag="late_bf16", align_bytes=64)
+        w2_bf_last = keep.tile([P, P, PACK], BF16, name="w2_bf_last", tag="top0", align_bytes=64)
+        for b in (1, 2):
             cols = slice((b - 1) * P, b * P)
-            round_w2(w2_bf_rest[:, cols, :], w2_rest[:, :, cols])
-        for b in range(1, PACK):
-            quantise_w2(b, w2_bf_rest[:, (b - 1) * P : b * P, :])
-        for b in range(1, PACK):
-            second_product(b)
+            round_w2(nc.scalar.copy, w2_bf_mid[:, cols, :], w2_rest[:, :, cols])
+        for b in (1, 2):
+            quantise_w2(b, w2_bf_mid[:, (b - 1) * P : b * P, :])
+        round_w2(nc.vector.tensor_copy, w2_bf_last[:], w2_rest[:, :, 2 * P :])
+        second_product(1)
+        quantise_w2(3, w2_bf_last[:])
+        second_product(2)
+        second_product(3)
 
         per = PIECE // MEMBERS
         pieces = G // PIECE
@@ -205,7 +248,7 @@ def tile_picked_layorderegs_none_p_kernel(
         pair_sums = [keep.tile([P, S, 2], F32, name=f"pair_sums{b}") for b in range(PACK)]
 
         def members(b, c):
-            ea = ring.tile([P, per, MEMBERS], F32, name="ea", bufs=4)
+            ea = ring.tile([P, per, MEMBERS], F32, name="ea", bufs=5)
             nc.scalar.activation(
                 ea[:].rearrange("p j t -> p (j t)"),
                 rows[b][:].indirect(n3_sb[:, c * PIECE // 16 : (c + 1) * PIECE // 16]),
@@ -227,43 +270,65 @@ def tile_picked_layorderegs_none_p_kernel(
             prod4 = [ring.tile([P, 64], F32, name=f"prod4{u}") for u in range(2)]
             inv4 = [ring.tile([P, 64], F32, name=f"inv4{u}") for u in range(2)]
             inv2 = [ring.tile([P, 2, 64], F32, name=f"inv2{u}") for u in range(2)]
-            inv1 = [ring.tile([P, 2, 128], F32, name=f"inv1{u}") for u in range(2)]
-            res = ring.tile([P, S], F32, name="res")
-            for u in range(2):
+            num = [ring.tile([P, 2, 128], F32, name=f"num{u}") for u in range(2)]
+            res = [ring.tile([P, 2, 128], F32, name=f"res{u}") for u in range(2)]
+
+            def denominators(u):
                 sums = pair_sums[b][:, u * half : (u + 1) * half, :]
                 nc.vector.scalar_tensor_tensor(
                     den[u][:].rearrange("p v j -> p (v j)"), sums[:, :, 0], 0.5, sums[:, :, 1], ALU.add, ALU.add
                 )
-            for u in range(2):
+
+            def products_of_two(u):
                 nc.vector.tensor_tensor(
                     prod2[u][:].rearrange("p v j -> p (v j)"), den[u][:, 0, :], den[u][:, 1, :], ALU.mult
                 )
-            next_members(b, 0)
-            for u in range(2):
+
+            def numerators(u):
+                nc.vector.scalar_tensor_tensor(
+                    num[u][:],
+                    banks[2 * b + u][:, :half].rearrange("p (v j) -> p v j", v=2),
+                    1.5,
+                    den[u][:, ::-1, :],
+                    ALU.mult,
+                    ALU.mult,
+                )
+
+            def products_of_four(u):
                 nc.vector.tensor_tensor(prod4[u][:], prod2[u][:, 0, :], prod2[u][:, 1, :], ALU.mult)
-            for u in range(2):
-                nc.vector.reciprocal(inv4[u][:], prod4[u][:])
-            for u in range(2):
+
+            def inverses_of_two(u):
                 nc.vector.tensor_tensor(
                     inv2[u][:], prod2[u][:, ::-1, :], inv4[u][:].unsqueeze(1).to_broadcast([P, 2, 64]), ALU.mult
                 )
-            next_members(b, 1)
-            for u in range(2):
+
+            def results(u):
                 nc.vector.tensor_tensor(
-                    inv1[u][:],
-                    den[u][:, ::-1, :],
+                    res[u][:],
+                    num[u][:],
                     inv2[u][:].rearrange("p v j -> p (v j)").unsqueeze(1).to_broadcast([P, 2, 128]),
                     ALU.mult,
                 )
-            for u in range(2):
-                nc.vector.scalar_tensor_tensor(
-                    res[:, u * half : (u + 1) * half],
-                    banks[2 * b + u][:, :half],
-                    1.5,
-                    inv1[u][:].rearrange("p v j -> p (v j)"),
-                    ALU.mult,
-                    ALU.mult,
+                nc.sync.dma_start(
+                    out_rows[:, b, u * half : (u + 1) * half], res[u][:].rearrange("p v j -> p (v j)")
                 )
-                nc.sync.dma_start(out_rows[:, b, u * half : (u + 1) * half], res[:, u * half : (u + 1) * half])
+
+            denominators(0)
+            denominators(1)
+            products_of_two(0)
+            numerators(0)
+            products_of_two(1)
+            products_of_four(0)
+            numerators(1)
+            products_of_four(1)
+            for u in range(2):
+                nc.vector.reciprocal(inv4[u][:], prod4[u][:])
+                if u == 0:
+                    next_members(b, 0)
+            inverses_of_two(0)
+            next_members(b, 1)
+            inverses_of_two(1)
+            results(0)
             next_members(b, 2)
+            results(1)
             next_members(b, 3)

@@ -18,7 +18,8 @@ ACT = mybir.ActivationFunctionType
 P = 128
 PACK = 4
 MEMBERS = 4
-PIECE = 512
+VECTOR_SHARE = 64
+VECTOR_COLUMNS = 320
 
 
 def tile_picked_layorderegs_none_p_kernel(
@@ -106,7 +107,7 @@ def tile_picked_layorderegs_none_p_kernel(
         round_w2(nc.scalar.copy, w2_bf_first[:], w2_first[:])
 
         banks = [psum.tile([P, S], F32, name=f"bank{b}") for b in range(8)]
-        rows = [keep.tile([P, 2 * S], F32, name=f"rows{t}") for t in range(PACK)]
+        rows = [keep.tile([P, 4 * S], F32, name=f"rows{t}") for t in range(PACK)]
         z_planes = keep.tile([P, PACK, S], BF16, name="z_planes", tag="late_bf16", align_bytes=64)
 
         def first_product(t, bank, cols):
@@ -126,31 +127,30 @@ def tile_picked_layorderegs_none_p_kernel(
             copy(rows[0][:, S + u * half : S + (u + 1) * half], banks[u][:, :half])
         for t in range(1, PACK):
             first_product(t, banks[1 + t][:], slice(0, S))
-            nc.scalar.copy(rows[t][:, S:], banks[1 + t][:])
+            nc.scalar.copy(rows[t][:, S : 2 * S], banks[1 + t][:])
 
-        pa = [keep.tile([P, W], F32, name=f"pa{t}") for t in range(PACK)]
-        pb = [keep.tile([P, W], F32, name=f"pb{t}") for t in range(PACK)]
-        ra = [keep.tile([P, W], F32, name=f"ra{t}") for t in range(PACK)]
-        rb = [keep.tile([P, W], F32, name=f"rb{t}") for t in range(PACK)]
+        pa, pb, ra, rb = ([rows[t][:, 2 * S + i * W : 2 * S + (i + 1) * W] for t in range(PACK)] for i in range(4))
         sorted_rows = [keep.tile([P, S], F32, name=f"dt{t}") for t in range(PACK)]
 
         def fetch_a(t):
-            nc.vector.tensor_copy(pa[t][:], rows[t][:, S:].indirect(n1_sb[:]))
+            nc.vector.tensor_copy(pa[t], rows[t][:, S : 2 * S].indirect(n1_sb[:]))
 
         def fetch_b(t):
-            nc.vector.tensor_copy(pb[t][:], rows[t][:, S:].indirect(n2_sb[:]))
+            nc.vector.tensor_copy(pb[t], rows[t][:, S : 2 * S].indirect(n2_sb[:]))
 
-        def put(t, values, places):
-            if t < PACK - 1:
-                nc.scalar.activation(sorted_rows[t][:].indirect(places[:]), values[:], ACT.Copy)
-            else:
-                nc.vector.tensor_copy(sorted_rows[t][:].indirect(places[:]), values[:])
+        def put_scalar(t, values, places, lo=0, hi=W):
+            nc.scalar.activation(
+                sorted_rows[t][:].indirect(places[:, lo // 16 : hi // 16]), values[:, lo:hi], ACT.Copy
+            )
+
+        def put_vector(t, values, places, lo=0, hi=W):
+            nc.vector.tensor_copy(sorted_rows[t][:].indirect(places[:, lo // 16 : hi // 16]), values[:, lo:hi])
 
         def larger(t):
-            nc.vector.tensor_tensor(ra[t][:], pa[t][:], pb[t][:], ALU.max)
+            nc.vector.tensor_tensor(ra[t], pa[t], pb[t], ALU.max)
 
         def smaller(t):
-            nc.vector.tensor_tensor(rb[t][:], pa[t][:], pb[t][:], ALU.min)
+            nc.vector.tensor_tensor(rb[t], pa[t], pb[t], ALU.min)
 
         def apply_gain(t):
             nc.vector.tensor_scalar(z_planes[:, t, :], sorted_rows[t][:], gn_sb[:, t : t + 1], None, ALU.mult)
@@ -166,28 +166,39 @@ def tile_picked_layorderegs_none_p_kernel(
             if 0 < t < PACK - 1:
                 smaller(t - 1)
         smaller(PACK - 1)
-        for t in range(PACK - 1):
-            put(t, ra[t], n1_sb)
-            if t > 0:
-                put(t - 1, rb[t - 1], n2_sb)
-        put(PACK - 2, rb[PACK - 2], n2_sb)
-        put(PACK - 1, ra[PACK - 1], n1_sb)
-        apply_gain(0)
-        put(PACK - 1, rb[PACK - 1], n2_sb)
+        put_scalar(0, ra[0], n1_sb)
+        put_scalar(1, ra[1], n1_sb)
+        put_scalar(0, rb[0], n2_sb, 0, W - VECTOR_SHARE)
+        put_scalar(2, ra[2], n1_sb)
+        put_scalar(1, rb[1], n2_sb)
+        put_scalar(2, rb[2], n2_sb)
+        put_vector(3, ra[3], n1_sb)
+        put_vector(0, rb[0], n2_sb, W - VECTOR_SHARE, W)
+        put_vector(3, rb[3], n2_sb)
+        for t in range(2):
+            nc.gpsimd.tensor_scalar(
+                z_planes[:, t, :], sorted_rows[t][:], gn_sb[:, t : t + 1], 0.0, ALU.mult, ALU.add
+            )
 
         quantise_w2(0, w2_bf_first[:])
         neg_tau = keep.tile([P, PACK], F32, name="neg_tau")
         nc.gpsimd.tensor_scalar(neg_tau[:], tau_sb, -1.0, 0.0, ALU.mult, ALU.add)
-        apply_gain(1)
         apply_gain(3)
-        nc.vector.tensor_scalar(z_planes[:, 2, :half], sorted_rows[2][:, :half], gn_sb[:, 2:3], None, ALU.mult)
-        nc.scalar.activation(z_planes[:, 2, half:], sorted_rows[2][:, half:], ACT.Copy, scale=gn_sb[:, 2:3])
+        for cols in (slice(0, P), slice(P, VECTOR_COLUMNS)):
+            nc.vector.tensor_scalar(z_planes[:, 2, cols], sorted_rows[2][:, cols], gn_sb[:, 2:3], None, ALU.mult)
+        nc.scalar.activation(
+            z_planes[:, 2, VECTOR_COLUMNS:], sorted_rows[2][:, VECTOR_COLUMNS:], ACT.Copy, scale=gn_sb[:, 2:3]
+        )
 
         z_bf = keep.tile([P, S, PACK], BF16, name="z_bf", align_bytes=64)
         z_words = [keep.tile([P, half], U32, name=f"z_words{u}", align_bytes=64) for u in range(2)]
         z_scales = [keep.tile([P, half], U8, name=f"z_scales{u}", align_bytes=64) for u in range(2)]
-        for u, copy in enumerate((nc.vector.tensor_copy, nc.scalar.copy)):
-            cols = slice(u * half, (u + 1) * half)
+        for cols, copy in (
+            (slice(0, P), nc.vector.tensor_copy),
+            (slice(P, half), nc.vector.tensor_copy),
+            (slice(half, VECTOR_COLUMNS), nc.vector.tensor_copy),
+            (slice(VECTOR_COLUMNS, S), nc.scalar.copy),
+        ):
             copy(
                 z_bf[:, cols, :].rearrange("p (c i) t -> p c t i", i=4),
                 z_planes[:, :, cols].rearrange("p t (c i) -> p c t i", i=4),
@@ -242,28 +253,29 @@ def tile_picked_layorderegs_none_p_kernel(
         second_product(2)
         second_product(3)
 
-        per = PIECE // MEMBERS
-        pieces = G // PIECE
         out_rows = out.rearrange("(b p) j -> p b j", p=P)
         pair_sums = [keep.tile([P, S, 2], F32, name=f"pair_sums{b}") for b in range(PACK)]
 
-        def members(b, c):
-            ea = ring.tile([P, per, MEMBERS], F32, name="ea", bufs=5)
+        def members(b, lo, hi):
+            ea = ring.tile([P, hi - lo, MEMBERS], F32, name="ea", bufs=3)
             nc.scalar.activation(
                 ea[:].rearrange("p j t -> p (j t)"),
-                rows[b][:].indirect(n3_sb[:, c * PIECE // 16 : (c + 1) * PIECE // 16]),
+                rows[b][:].indirect(n3_sb[:, lo * MEMBERS // 16 : hi * MEMBERS // 16]),
                 ACT.Exp,
                 bias=bias[:, b : b + 1],
                 scale=tau_sb[:, b : b + 1],
             )
-            nc.vector.tensor_tensor(pair_sums[b][:, c * per : (c + 1) * per, :], ea[:, :, 0:2], ea[:, :, 2:4], ALU.add)
+            nc.vector.tensor_tensor(pair_sums[b][:, lo:hi, :], ea[:, :, 0:2], ea[:, :, 2:4], ALU.add)
 
-        def next_members(b, c):
-            if b + 1 < PACK:
-                members(b + 1, c)
+        def members_of_half(b, u):
+            if b == PACK - 1 and u == 1:
+                members(b, half, half + P)
+                members(b, half + P, S)
+            elif b < PACK:
+                members(b, u * half, (u + 1) * half)
 
-        for c in range(pieces):
-            members(0, c)
+        members_of_half(0, 0)
+        members_of_half(0, 1)
         for b in range(PACK):
             den = [ring.tile([P, 2, 128], F32, name=f"den{u}") for u in range(2)]
             prod2 = [ring.tile([P, 2, 64], F32, name=f"prod2{u}") for u in range(2)]
@@ -323,12 +335,9 @@ def tile_picked_layorderegs_none_p_kernel(
             products_of_four(1)
             for u in range(2):
                 nc.vector.reciprocal(inv4[u][:], prod4[u][:])
-                if u == 0:
-                    next_members(b, 0)
             inverses_of_two(0)
-            next_members(b, 1)
+            members_of_half(b + 1, 0)
             inverses_of_two(1)
             results(0)
-            next_members(b, 2)
             results(1)
-            next_members(b, 3)
+            members_of_half(b + 1, 1)

from contextlib import ExitStack

import concourse.mybir as mybir

K, T, S, N, H, W, G = 512, 2048, 512, 512, 512, 256, 2048
FLOPS = 2 * K * H * S + 2 * H * N * S

F32 = mybir.dt.float32
BF16 = mybir.dt.bfloat16
I32 = mybir.dt.int32
U32 = mybir.dt.uint32
U16 = mybir.dt.uint16
U8 = mybir.dt.uint8
FP8X4 = mybir.dt.float8_e4m3fn_x4
ALU = mybir.AluOpType
ACT = mybir.ActivationFunctionType

P = 128
PACK = 4
MEMBERS = 4
VECTOR_SHARE = 64
VECTOR_COLUMNS = 320


def tile_picked_layorderegs_none_p_kernel(
    tc, x_words, x_scales, w1, gn, w2, tau, offs, n1, n2, n3, out
):
    nc = tc.nc
    with ExitStack() as ctx:
        keep = ctx.enter_context(tc.tile_pool(name="keep", bufs=1))
        ring = ctx.enter_context(tc.tile_pool(name="ring", bufs=2))
        psum = ctx.enter_context(tc.psum_pool(name="psum", bufs=1))

        offs_sb = keep.tile([P, S // 16], U16, name="offs_sb")
        n1_sb = keep.tile([P, W // 16], U16, name="n1_sb")
        n2_sb = keep.tile([P, W // 16], U16, name="n2_sb")
        n3_sb = keep.tile([P, G // 16], U16, name="n3_sb")
        xw = keep.tile([P, T], I32, name="xw", tag="x_then_w2", align_bytes=64)
        xs = keep.tile([P, T], U8, name="xs", align_bytes=64)
        half = H // 2
        w1_raw = keep.tile([P, PACK, H], F32, name="w1_raw", tag="w1_then_w2")

        nc.vector.memset(xs[:].bitcast(I32), 0)
        nc.sync.dma_start(offs_sb[:], offs)
        nc.sync.dma_start(n1_sb[:], n1)
        nc.sync.dma_start(w1_raw[:], w1.rearrange("(p j) c -> p j c", j=PACK))
        for q in range(4):
            nc.sync.dma_start(
                xs[32 * q : 32 * q + 4, :].bitcast(I32), x_scales[0, 4 * q : 4 * q + 4, :].bitcast(I32)
            )
        nc.sync.dma_start(n2_sb[:], n2)
        nc.sync.dma_start(n3_sb[:], n3)
        nc.sync.dma_start(xw[:], x_words[0].rearrange("p n t -> p (n t)").bitcast(I32))

        w1_bf = keep.tile([P, PACK, P, PACK], BF16, name="w1_bf", tag="w1_then_rows", align_bytes=64)
        for u, copy in enumerate((nc.scalar.copy, nc.vector.tensor_copy)):
            copy(
                w1_bf[:, :, u * 64 : (u + 1) * 64, :].rearrange("p t m j -> p m j t"),
                w1_raw[:, :, u * half : (u + 1) * half].rearrange("p j (m t) -> p m j t", t=PACK),
            )
        w1_words = keep.tile([P, H], U32, name="w1_words", align_bytes=64)
        w1_scales = keep.tile([P, H], U8, name="w1_scales", align_bytes=64)

        def quantise_w1(t):
            cols = slice(t * P, (t + 1) * P)
            nc.vector.quantize_mx(
                out=w1_words[:, cols].bitcast(FP8X4),
                scales=w1_scales[:, cols],
                in_=w1_bf[:, t, :, :].rearrange("p m j -> p (m j)"),
            )

        xq_words = keep.tile([P, S], U32, name="xq_words", align_bytes=64)
        xq_scales = keep.tile([P, S], U8, name="xq_scales", align_bytes=64)
        for t in range(PACK):
            quantise_w1(t)
        nc.vector.tensor_copy(xq_scales[:], xs[:].indirect(offs_sb[:]))
        for u in range(2):
            nc.vector.tensor_copy(
                xq_words[:, u * half : (u + 1) * half],
                xw[:].bitcast(U32).indirect(offs_sb[:, u * half // 16 : (u + 1) * half // 16]),
            )

        w2_rows = w2.rearrange("(p j) c -> p j c", j=PACK)
        w2_first = keep.tile([P, PACK, P], F32, name="w2_first", tag="w1_then_w2")
        w2_rest = keep.tile([P, PACK, N - P], F32, name="w2_rest", tag="x_then_w2", align_bytes=64)
        per_row = keep.tile([P, 16], F32, name="per_row", tag="w1_then_rows", align_bytes=64)
        gn_sb = per_row[:, 0:PACK]
        tau_sb = per_row[:, 8 : 8 + PACK]
        nc.sync.dma_start(w2_first[:], w2_rows[:, :, :P])
        nc.sync.dma_start(gn_sb, gn.rearrange("(p t) o -> p (t o)", t=PACK))
        with nc.allow_non_contiguous_dma(reason="one rate a partition for each block of 128 rows"):
            nc.sync.dma_start(tau_sb, tau.rearrange("(b p) o -> p (b o)", p=P))
        nc.sync.dma_start(w2_rest[:], w2_rows[:, :, P:])

        w2_words = [keep.tile([P, P], U32, name=f"w2_words{b}", align_bytes=64) for b in range(PACK)]
        w2_scales = [keep.tile([P, P], U8, name=f"w2_scales{b}", align_bytes=64) for b in range(PACK)]

        def round_w2(copy, grouped, raw):
            copy(grouped.rearrange("p (c i) j -> p c j i", i=4), raw.rearrange("p j (c i) -> p c j i", i=4))

        def quantise_w2(b, grouped):
            nc.vector.quantize_mx(
                out=w2_words[b][:].bitcast(FP8X4), scales=w2_scales[b][:], in_=grouped.rearrange("p m j -> p (m j)")
            )

        w2_bf_first = keep.tile([P, P, PACK], BF16, name="w2_bf_first", align_bytes=64)
        round_w2(nc.scalar.copy, w2_bf_first[:], w2_first[:])

        banks = [psum.tile([P, S], F32, name=f"bank{b}") for b in range(8)]
        rows = [keep.tile([P, 4 * S], F32, name=f"rows{t}") for t in range(PACK)]
        z_planes = keep.tile([P, PACK, S], BF16, name="z_planes", tag="late_bf16", align_bytes=64)

        def first_product(t, bank, cols):
            rows_t = slice(t * P, (t + 1) * P)
            nc.tensor.matmul_mx(
                out=bank,
                lhsT=w1_words[:, rows_t].bitcast(FP8X4),
                lhsT_scale=w1_scales[:, rows_t],
                rhs=xq_words[:, cols].bitcast(FP8X4),
                rhs_scale=xq_scales[:, cols],
                start=True,
                stop=True,
            )

        for u, copy in enumerate((nc.scalar.copy, nc.vector.tensor_copy)):
            first_product(0, banks[u][:, :half], slice(u * half, (u + 1) * half))
            copy(rows[0][:, S + u * half : S + (u + 1) * half], banks[u][:, :half])
        for t in range(1, PACK):
            first_product(t, banks[1 + t][:], slice(0, S))
            nc.scalar.copy(rows[t][:, S : 2 * S], banks[1 + t][:])

        pa, pb, ra, rb = ([rows[t][:, 2 * S + i * W : 2 * S + (i + 1) * W] for t in range(PACK)] for i in range(4))
        sorted_rows = [keep.tile([P, S], F32, name=f"dt{t}") for t in range(PACK)]

        def fetch_a(t):
            nc.vector.tensor_copy(pa[t], rows[t][:, S : 2 * S].indirect(n1_sb[:]))

        def fetch_b(t):
            nc.vector.tensor_copy(pb[t], rows[t][:, S : 2 * S].indirect(n2_sb[:]))

        def put_scalar(t, values, places, lo=0, hi=W):
            nc.scalar.activation(
                sorted_rows[t][:].indirect(places[:, lo // 16 : hi // 16]), values[:, lo:hi], ACT.Copy
            )

        def put_vector(t, values, places, lo=0, hi=W):
            nc.vector.tensor_copy(sorted_rows[t][:].indirect(places[:, lo // 16 : hi // 16]), values[:, lo:hi])

        def larger(t):
            nc.vector.tensor_tensor(ra[t], pa[t], pb[t], ALU.max)

        def smaller(t):
            nc.vector.tensor_tensor(rb[t], pa[t], pb[t], ALU.min)

        def apply_gain(t):
            nc.vector.tensor_scalar(z_planes[:, t, :], sorted_rows[t][:], gn_sb[:, t : t + 1], None, ALU.mult)

        fetch_a(0)
        for t in range(PACK):
            fetch_b(t)
            if t + 1 < PACK:
                fetch_a(t + 1)
            else:
                smaller(t - 1)
            larger(t)
            if 0 < t < PACK - 1:
                smaller(t - 1)
        smaller(PACK - 1)
        put_scalar(0, ra[0], n1_sb)
        put_scalar(1, ra[1], n1_sb)
        put_scalar(0, rb[0], n2_sb, 0, W - VECTOR_SHARE)
        put_scalar(2, ra[2], n1_sb)
        put_scalar(1, rb[1], n2_sb)
        put_scalar(2, rb[2], n2_sb)
        put_vector(3, ra[3], n1_sb)
        put_vector(0, rb[0], n2_sb, W - VECTOR_SHARE, W)
        put_vector(3, rb[3], n2_sb)
        for t in range(2):
            nc.gpsimd.tensor_scalar(
                z_planes[:, t, :], sorted_rows[t][:], gn_sb[:, t : t + 1], 0.0, ALU.mult, ALU.add
            )

        quantise_w2(0, w2_bf_first[:])
        neg_tau = keep.tile([P, PACK], F32, name="neg_tau")
        nc.gpsimd.tensor_scalar(neg_tau[:], tau_sb, -1.0, 0.0, ALU.mult, ALU.add)
        apply_gain(3)
        for cols in (slice(0, P), slice(P, VECTOR_COLUMNS)):
            nc.vector.tensor_scalar(z_planes[:, 2, cols], sorted_rows[2][:, cols], gn_sb[:, 2:3], None, ALU.mult)
        nc.scalar.activation(
            z_planes[:, 2, VECTOR_COLUMNS:], sorted_rows[2][:, VECTOR_COLUMNS:], ACT.Copy, scale=gn_sb[:, 2:3]
        )

        z_bf = keep.tile([P, S, PACK], BF16, name="z_bf", align_bytes=64)
        z_words = [keep.tile([P, half], U32, name=f"z_words{u}", align_bytes=64) for u in range(2)]
        z_scales = [keep.tile([P, half], U8, name=f"z_scales{u}", align_bytes=64) for u in range(2)]
        for cols, copy in (
            (slice(0, P), nc.vector.tensor_copy),
            (slice(P, half), nc.vector.tensor_copy),
            (slice(half, VECTOR_COLUMNS), nc.vector.tensor_copy),
            (slice(VECTOR_COLUMNS, S), nc.scalar.copy),
        ):
            copy(
                z_bf[:, cols, :].rearrange("p (c i) t -> p c t i", i=4),
                z_planes[:, :, cols].rearrange("p t (c i) -> p c t i", i=4),
            )
        for u in range(2):
            cols = slice(u * half, (u + 1) * half)
            nc.vector.quantize_mx(
                out=z_words[u][:].bitcast(FP8X4),
                scales=z_scales[u][:],
                in_=z_bf[:, cols, :].rearrange("p c t -> p (c t)"),
            )

        top = [keep.tile([P, 2], F32, name=f"top{b}", tag=f"top{b}", align_bytes=64) for b in range(PACK)]
        bias = keep.tile([P, PACK], F32, name="bias")

        def second_product(b):
            for u in range(2):
                bank = banks[2 * b + u]
                nc.tensor.matmul_mx(
                    out=bank[:, :half],
                    lhsT=w2_words[b][:].bitcast(FP8X4),
                    lhsT_scale=w2_scales[b][:],
                    rhs=z_words[u][:].bitcast(FP8X4),
                    rhs_scale=z_scales[u][:],
                    start=True,
                    stop=True,
                )
                nc.vector.tensor_scalar(
                    rows[b][:, u * half : (u + 1) * half],
                    bank[:, :half],
                    1.0,
                    None,
                    ALU.mult,
                    ALU.max,
                    accum_out=top[b][:, u : u + 1],
                )
            nc.vector.tensor_scalar(
                bias[:, b : b + 1], top[b][:, 0:1], top[b][:, 1:2], neg_tau[:, b : b + 1], ALU.max, ALU.mult
            )

        second_product(0)
        w2_bf_mid = keep.tile([P, 2 * P, PACK], BF16, name="w2_bf_mid", tag="late_bf16", align_bytes=64)
        w2_bf_last = keep.tile([P, P, PACK], BF16, name="w2_bf_last", tag="top0", align_bytes=64)
        for b in (1, 2):
            cols = slice((b - 1) * P, b * P)
            round_w2(nc.scalar.copy, w2_bf_mid[:, cols, :], w2_rest[:, :, cols])
        for b in (1, 2):
            quantise_w2(b, w2_bf_mid[:, (b - 1) * P : b * P, :])
        round_w2(nc.vector.tensor_copy, w2_bf_last[:], w2_rest[:, :, 2 * P :])
        second_product(1)
        quantise_w2(3, w2_bf_last[:])
        second_product(2)
        second_product(3)

        out_rows = out.rearrange("(b p) j -> p b j", p=P)
        pair_sums = [keep.tile([P, S, 2], F32, name=f"pair_sums{b}") for b in range(PACK)]

        def members(b, lo, hi):
            ea = ring.tile([P, hi - lo, MEMBERS], F32, name="ea", bufs=3)
            nc.scalar.activation(
                ea[:].rearrange("p j t -> p (j t)"),
                rows[b][:].indirect(n3_sb[:, lo * MEMBERS // 16 : hi * MEMBERS // 16]),
                ACT.Exp,
                bias=bias[:, b : b + 1],
                scale=tau_sb[:, b : b + 1],
            )
            nc.vector.tensor_tensor(pair_sums[b][:, lo:hi, :], ea[:, :, 0:2], ea[:, :, 2:4], ALU.add)

        def members_of_half(b, u):
            if b == PACK - 1 and u == 1:
                members(b, half, half + P)
                members(b, half + P, S)
            elif b < PACK:
                members(b, u * half, (u + 1) * half)

        members_of_half(0, 0)
        members_of_half(0, 1)
        for b in range(PACK):
            den = [ring.tile([P, 2, 128], F32, name=f"den{u}") for u in range(2)]
            prod2 = [ring.tile([P, 2, 64], F32, name=f"prod2{u}") for u in range(2)]
            prod4 = [ring.tile([P, 64], F32, name=f"prod4{u}") for u in range(2)]
            inv4 = [ring.tile([P, 64], F32, name=f"inv4{u}") for u in range(2)]
            inv2 = [ring.tile([P, 2, 64], F32, name=f"inv2{u}") for u in range(2)]
            num = [ring.tile([P, 2, 128], F32, name=f"num{u}") for u in range(2)]
            res = [ring.tile([P, 2, 128], F32, name=f"res{u}") for u in range(2)]

            def denominators(u):
                sums = pair_sums[b][:, u * half : (u + 1) * half, :]
                nc.vector.scalar_tensor_tensor(
                    den[u][:].rearrange("p v j -> p (v j)"), sums[:, :, 0], 0.5, sums[:, :, 1], ALU.add, ALU.add
                )

            def products_of_two(u):
                nc.vector.tensor_tensor(
                    prod2[u][:].rearrange("p v j -> p (v j)"), den[u][:, 0, :], den[u][:, 1, :], ALU.mult
                )

            def numerators(u):
                nc.vector.scalar_tensor_tensor(
                    num[u][:],
                    banks[2 * b + u][:, :half].rearrange("p (v j) -> p v j", v=2),
                    1.5,
                    den[u][:, ::-1, :],
                    ALU.mult,
                    ALU.mult,
                )

            def products_of_four(u):
                nc.vector.tensor_tensor(prod4[u][:], prod2[u][:, 0, :], prod2[u][:, 1, :], ALU.mult)

            def inverses_of_two(u):
                nc.vector.tensor_tensor(
                    inv2[u][:], prod2[u][:, ::-1, :], inv4[u][:].unsqueeze(1).to_broadcast([P, 2, 64]), ALU.mult
                )

            def results(u):
                nc.vector.tensor_tensor(
                    res[u][:],
                    num[u][:],
                    inv2[u][:].rearrange("p v j -> p (v j)").unsqueeze(1).to_broadcast([P, 2, 128]),
                    ALU.mult,
                )
                nc.sync.dma_start(
                    out_rows[:, b, u * half : (u + 1) * half], res[u][:].rearrange("p v j -> p (v j)")
                )

            denominators(0)
            denominators(1)
            products_of_two(0)
            numerators(0)
            products_of_two(1)
            products_of_four(0)
            numerators(1)
            products_of_four(1)
            for u in range(2):
                nc.vector.reciprocal(inv4[u][:], prod4[u][:])
            inverses_of_two(0)
            members_of_half(b + 1, 0)
            inverses_of_two(1)
            results(0)
            results(1)
            members_of_half(b + 1, 1)
